import numpy as np
import ml_dtypes


def mxq(x, axis, fmt="e4m3"):
    dtype, down = {"e4m3": (ml_dtypes.float8_e4m3fn, 7), "e5m2": (ml_dtypes.float8_e5m2, 14)}[fmt]
    v = np.moveaxis(np.asarray(x, np.float32).astype(ml_dtypes.bfloat16).astype(np.float64), axis, -1)
    blocks = v.reshape(v.shape[:-1] + (-1, 32))
    amax = np.abs(blocks).max(-1, keepdims=True)
    byte = np.maximum(np.where(amax > 0, np.frexp(amax)[1] - 1 + 127, 0) - down, 1)
    scale = np.exp2(byte - 127.0)
    codes = (blocks / scale).astype(np.float32).astype(dtype).astype(np.float64)
    return np.moveaxis((codes * scale).reshape(v.shape), -1, axis)


WIDE = False


def mx_kscale(k):
    if not WIDE:
        return np.ones(k)
    levels = np.array([10, -10, 5, -5, 0])
    if k % 512:
        return np.exp2(np.random.permutation(np.resize(levels, k // 32))).repeat(32)
    a = np.empty((k // 512, 16))
    for p in range(k // 512):
        a[p, :8] = np.random.permutation(np.resize(levels, 8))
        for g in range(8):
            far = levels[np.abs(levels - a[p, g]) >= 10]
            a[p, g + 8] = far[np.random.randint(len(far))]
    return np.exp2(a.ravel()).repeat(32)


def f64(x):
    return np.asarray(x).astype(np.float64)


def striped(idx):
    return np.tile(np.asarray(idx).reshape(-1, 16).T, (8, 1)).astype(np.uint16)


def unstriped(offs):
    return offs[:16].T.reshape(-1).astype(np.int64)


E2M1 = np.array([0.0, 0.5, 1.0, 1.5, 2.0, 3.0, 4.0, 6.0, -0.0, -0.5, -1.0, -1.5, -2.0, -3.0, -4.0, -6.0])


def pack_weight(w, fmt):
    k, n = w.shape
    w = f64(np.asarray(w, np.float32).astype(ml_dtypes.bfloat16)).reshape(k // 32, 32, n)
    amax = np.abs(w).max(1)
    if fmt == "e4m3":
        byte = np.frexp(amax)[1] - 1 + 127 - 7
    else:
        mant, ex = np.frexp(amax / 6.0)
        byte = np.where(mant > 0.5, ex, ex - 1) + 127
    byte = np.clip(np.where(amax > 0, byte, 1), 1, 254)
    scaled = (w * np.exp2(127.0 - byte)[:, None, :]).reshape(k, n).astype(np.float32)
    by_word = np.ascontiguousarray(scaled.reshape(k // 512, 128, 4, n).transpose(0, 1, 3, 2))
    if fmt == "e4m3":
        words = by_word.astype(ml_dtypes.float8_e4m3fn).view(np.uint8)
    else:
        c = by_word.astype(ml_dtypes.float4_e2m1fn).view(np.uint8) & 0xF
        words = (c[..., 0::2] | (c[..., 1::2] << 4)).reshape(k // 512, 128, 2 * n)
    return np.ascontiguousarray(words), np.ascontiguousarray(byte.astype(np.uint8).reshape(k // 512, 16, n))


def unpack_weight(words, scales, fmt):
    g, _, n = scales.shape
    words = np.ascontiguousarray(words).reshape(g, 128, n, -1)
    if fmt == "e4m3":
        vals = words.view(ml_dtypes.float8_e4m3fn).astype(np.float64)
    else:
        nib = np.empty((g, 128, n, 4), np.uint8)
        nib[..., 0::2] = words & 0xF
        nib[..., 1::2] = words >> 4
        vals = E2M1[nib]
    vals = vals * np.repeat(np.exp2(scales.astype(np.float64) - 127.0), 8, axis=1)[..., None]
    return vals.transpose(0, 1, 3, 2).reshape(g * 512, n)


def bf(x):
    return np.asarray(x, np.float32).astype(ml_dtypes.bfloat16)


def planes(Y):
    r, m = Y.shape
    b = f64(bf(Y)).reshape(r // 32, 32, m)
    amax = np.abs(b).max(1)
    byte = np.clip(np.where(amax > 0, np.frexp(amax)[1] - 1 + 127 - 7, 1), 1, 254)
    codes = (b * np.exp2(127.0 - byte)[:, None, :]).reshape(r, m).astype(np.float32).astype(ml_dtypes.float8_e4m3fn).view(np.uint8)
    words = codes.reshape(r // 512, 128, 4, m).transpose(0, 1, 3, 2)
    return np.ascontiguousarray(words), np.ascontiguousarray(byte.astype(np.uint8).reshape(r // 512, 16, m))


K, T, C, J, I = 1024, 1024, 1024, 512, 512


def setup_inputs():
    n = np.random.standard_normal
    idx = np.random.permutation(T)[:J]
    idx2 = np.random.permutation(C)[:I]
    fk = mx_kscale(K)
    wcp = pack_weight(n((K, C)) / fk[:, None], "e2m1")
    return {
        "xa": (n((K, T)) * 0.03 * fk[:, None]).astype(np.float32),
        "wc_words": wcp[0],
        "wc_scales": wcp[1],
        "cb": np.tile(0.5 * n(C), (128, 1)).astype(np.float32),
        "offs": striped(idx),
        "offs2": striped(idx2),
    }


def reference(xa, wc_words, wc_scales, cb, offs, offs2):
    idx = unstriped(offs)
    idx2 = unstriped(offs2)
    wcu = unpack_weight(wc_words, wc_scales, "e2m1")
    xaidxq = mxq(f64(xa)[:, idx], 0, "e4m3")
    wcidx2g = wcu[:, idx2]
    a = xaidxq.T @ wcidx2g
    y = np.tanh(a + f64(cb)[:1][:, idx2])
    words, scales = planes(y)
    return y, words, scales

@@ -1,0 +1,214 @@
+from contextlib import ExitStack
+
+import concourse.mybir as mybir
+from concourse.masks import make_identity
+
+K, T, C, J, I = 1024, 1024, 1024, 512, 512
+FLOPS = 2 * K * J * I
+BYTES = 4 * K * T + K * C // 2 + K * C // 32 + 4 * C + 2 * 2 * 128 * 32 + 4 * J * I + J * I + J * I // 32
+
+F32 = mybir.dt.float32
+BF16 = mybir.dt.bfloat16
+I32 = mybir.dt.int32
+U32 = mybir.dt.uint32
+U16 = mybir.dt.uint16
+U8 = mybir.dt.uint8
+FP8X4 = mybir.dt.float8_e4m3fn_x4
+FP4X4 = mybir.dt.float4_e2m1fn_x4
+TANH = mybir.ActivationFunctionType.Tanh
+ADD = mybir.AluOpType.add
+
+P = 128
+PACK = 4
+PASSES = K // (P * PACK)
+CHUNK = 512
+RING = 4
+LAST_SCALAR = 160
+CAST_SCALAR = 128
+
+
+def tile_list_picked_tokens_by_picked_classes_pl_kernel(
+    tc, xa, wc_words, wc_scales, cb, offs, offs2, out_0, out_1, out_2
+):
+    nc = tc.nc
+    with ExitStack() as ctx:
+        keep = ctx.enter_context(tc.tile_pool(name="keep", bufs=1))
+        ring = ctx.enter_context(tc.tile_pool(name="ring", bufs=RING))
+        psum = ctx.enter_context(tc.psum_pool(name="psum", bufs=1))
+
+        tok = keep.tile([P, J // 16], U16, name="tok")
+        cls = keep.tile([P, I // 16], U16, name="cls")
+        wwin = [keep.tile([P, C], U16, name=f"wwin{g}", align_bytes=64) for g in range(PASSES)]
+        swin = keep.tile([P, C], U8, name="swin", align_bytes=64)
+        cbwin = keep.tile([P, C], F32, name="cbwin")
+        raw = {}
+        win = [keep.tile([P, 2 * T], BF16, name=f"win{q}", align_bytes=64) for q in range(2 * PASSES)]
+        warm = keep.tile([P, 1], F32, name="warm")
+        warm2 = keep.tile([P, 1], F32, name="warm2")
+        ident = keep.tile([P, P], F32, name="ident")
+        s1 = keep.tile([P, I], U8, name="s1", align_bytes=64)
+
+        nc.gpsimd.memset(swin[:].bitcast(I32), 0)
+        nc.vector.memset(cbwin[:], 0.0)
+        nc.vector.memset(warm[:], 0.0)
+        nc.vector.memset(s1[:].bitcast(I32), 0)
+
+        xrows = xa.rearrange("(g p h e) t -> g h p e t", g=PASSES, p=P, h=2, e=2)
+
+        def load_x(n):
+            q, c = divmod(n, T // CHUNK)
+            raw[q, c] = ring.tile([P, 2, CHUNK], F32, name="raw")
+            nc.sync.dma_start(raw[q, c][:], xrows[q // 2, q % 2][:, :, c * CHUNK : (c + 1) * CHUNK])
+
+        nc.sync.dma_start(cls[:], offs2)
+        nc.sync.dma_start(wwin[0][:].bitcast(I32), wc_words[0].bitcast(I32))
+        load_x(0)
+        for Q in range(4):
+            nc.scalar.dma_start(
+                swin[32 * Q : 32 * Q + 4 * PASSES, :].bitcast(I32),
+                wc_scales[:, 4 * Q : 4 * Q + 4, :].bitcast(I32),
+            )
+        nc.sync.dma_start(wwin[1][:].bitcast(I32), wc_words[1].bitcast(I32))
+        load_x(1)
+        nc.sync.dma_start(tok[:], offs)
+        nc.scalar.dma_start(cbwin[0:1, :], cb[0:1, :])
+        for n in range(2, RING):
+            load_x(n)
+        nc.scalar.activation(warm2[:], warm[:], TANH)
+        make_identity(nc, ident[:])
+
+        wg = [keep.tile([P, I], U16, name=f"wg{g}", align_bytes=64) for g in range(PASSES)]
+        sg = keep.tile([P, I], U8, name="sg", align_bytes=64)
+        bias = keep.tile([P, I], F32, name="bias")
+        nc.vector.tensor_copy(wg[0][:], wwin[0][:].indirect(cls[:]))
+        nc.vector.tensor_copy(sg[:], swin[:].indirect(cls[:]))
+        for Q in range(4):
+            nc.gpsimd.dma_start(
+                s1[32 * Q : 32 * Q + 4, :].bitcast(I32), sg[32 * Q + 4 : 32 * Q + 8, :].bitcast(I32)
+            )
+        nc.vector.tensor_copy(wg[1][:], wwin[1][:].indirect(cls[:]))
+        biasrow = keep.tile([P, I], F32, name="biasrow")
+        biascol = keep.tile([P, I // P], F32, name="biascol")
+        nc.vector.tensor_copy(biasrow[:], cbwin[:].indirect(cls[:]))
+        turned = psum.tile([P, I // P, P], F32, name="turned")
+        spread = psum.tile([P, I // P, P], F32, name="spread")
+        for b in range(I // P):
+            nc.tensor.transpose(turned[:, b, :], biasrow[:, b * P : (b + 1) * P], ident[:])
+        nc.scalar.copy(biascol[:], turned[:, :, 0])
+        for b in range(I // P):
+            nc.tensor.transpose(spread[:, b, :], biascol[:, b : b + 1].to_broadcast([P, P]), ident[:])
+        wscale = [sg, s1]
+
+        def cast(eng, q, lo, hi):
+            c, at = divmod(lo, CHUNK)
+            eng(
+                win[q][:, 2 * lo : 2 * hi].rearrange("p (t e) -> p t e", e=2),
+                raw[q, c][:, :, at : at + hi - lo].rearrange("p e t -> p t e"),
+            )
+
+        HALF = J // 2
+        picked = [
+            [keep.tile([P, 2, HALF], F32, name=f"picked{g}_{s}") for s in range(2)] for g in range(PASSES)
+        ]
+        grouped = [keep.tile([P, PACK * J], BF16, name=f"grouped{g}", align_bytes=64) for g in range(PASSES)]
+        codes = [keep.tile([P, J], U32, name=f"codes{g}", align_bytes=64) for g in range(PASSES)]
+        scales = [keep.tile([P, J], U8, name=f"scales{g}", align_bytes=64) for g in range(PASSES)]
+        acc = [psum.tile([P, I], F32, name=f"acc{t}") for t in range(PACK)]
+
+        def gather(q, s):
+            nc.vector.tensor_copy(
+                picked[q // 2][s][:, q % 2, :],
+                win[q][:].bitcast(F32).indirect(tok[:, s * 16 : (s + 1) * 16]),
+            )
+
+        def weave(eng, g, s):
+            eng(
+                grouped[g][:].bitcast(F32).rearrange("p (t m h) -> p m h t", t=PACK, h=2)[
+                    :, s * 64 : (s + 1) * 64
+                ],
+                picked[g][s][:].rearrange("p h (m t) -> p m h t", t=PACK),
+            )
+
+        def quant(g, lo, hi):
+            nc.vector.quantize_mx(
+                out=codes[g][:, lo:hi].bitcast(FP8X4),
+                scales=scales[g][:, lo:hi],
+                in_=grouped[g][:, PACK * lo : PACK * hi],
+            )
+
+        def mm(g, t):
+            nc.tensor.matmul_mx(
+                out=acc[t][:],
+                lhsT=codes[g][:, t * P : (t + 1) * P].bitcast(FP8X4),
+                lhsT_scale=scales[g][:, t * P : (t + 1) * P],
+                rhs=wg[g][:].bitcast(FP4X4),
+                rhs_scale=wscale[g][:],
+                start=(g == 0),
+                stop=(g == PASSES - 1),
+            )
+
+        for q in range(3):
+            for c in range(2):
+                cast(nc.scalar.copy, q, c * CHUNK, (c + 1) * CHUNK)
+                if 2 * q + c + RING < 8:
+                    load_x(2 * q + c + RING)
+            gather(q, 0)
+            gather(q, 1)
+            if q == 1:
+                weave(nc.vector.tensor_copy, 0, 0)
+                weave(nc.vector.tensor_copy, 0, 1)
+                quant(0, 0, J)
+                for t in range(PACK):
+                    mm(0, t)
+        cast(nc.scalar.copy, 3, 0, CHUNK)
+        cast(nc.scalar.copy, 3, CHUNK, CHUNK + LAST_SCALAR)
+        cast(nc.vector.tensor_copy, 3, CHUNK + LAST_SCALAR, T)
+        gather(3, 0)
+        gather(3, 1)
+        weave(nc.scalar.copy, 1, 0)
+        weave(nc.vector.tensor_copy, 1, 1)
+        nc.scalar.copy(bias[:], spread[:].rearrange("p b n -> p (b n)"))
+        for t in range(PACK):
+            quant(1, t * P, (t + 1) * P)
+            mm(1, t)
+
+        y = keep.tile([P, PACK, I], F32, name="y")
+        z = [keep.tile([P, I], F32, name=f"z{t}") for t in range(PACK)]
+        yb = keep.tile([P, PACK * I], BF16, name="yb", align_bytes=64)
+        ycodes = keep.tile([P, I], U32, name="ycodes", align_bytes=64)
+        yscales = keep.tile([P, I], U8, name="yscales", align_bytes=64)
+        orows = out_0.rearrange("(p t) i -> p t i", t=PACK)
+        IH = I // 2
+        for t in range(PACK):
+            spans = [(0, I)] if t < PACK - 1 else [(0, IH), (IH, I)]
+            for lo, hi in spans:
+                nc.vector.tensor_tensor(z[t][:, lo:hi], acc[t][:, lo:hi], bias[:, lo:hi], ADD)
+                nc.scalar.activation(y[:, t, lo:hi], z[t][:, lo:hi], TANH)
+            nc.sync.dma_start(orows[:, t, :], y[:, t, :])
+
+        def ycast(eng, lo, hi):
+            eng(
+                yb[:, PACK * lo : PACK * hi].rearrange("p (c i t) -> p c t i", i=4, t=PACK),
+                y[:, :, lo:hi].rearrange("p t (c i) -> p c t i", i=4),
+            )
+
+        owords = out_1[0].rearrange("p c r -> p (c r)").bitcast(I32)
+
+        def yquant(lo, hi):
+            nc.vector.quantize_mx(
+                out=ycodes[:, lo:hi].bitcast(FP8X4),
+                scales=yscales[:, lo:hi],
+                in_=yb[:, PACK * lo : PACK * hi],
+            )
+            nc.sync.dma_start(owords[:, lo:hi], ycodes[:, lo:hi].bitcast(I32))
+
+        ycast(nc.vector.tensor_copy, 0, IH)
+        ycast(nc.scalar.copy, I - CAST_SCALAR, I)
+        ycast(nc.vector.tensor_copy, IH, I - CAST_SCALAR)
+        yquant(0, IH)
+        yquant(IH, I)
+        for Q in range(4):
+            eng = nc.sync if Q < 2 else nc.scalar
+            eng.dma_start(
+                out_2[0, 4 * Q : 4 * Q + 4, :].bitcast(I32), yscales[32 * Q : 32 * Q + 4, :].bitcast(I32)
+            )

@@ -22,9 +22,8 @@ P = 128
 PACK = 4
 PASSES = K // (P * PACK)
 CHUNK = 512
-RING = 4
 LAST_SCALAR = 160
-CAST_SCALAR = 128
+CAST_SCALAR = 160
 
 
 def tile_list_picked_tokens_by_picked_classes_pl_kernel(
@@ -33,7 +32,7 @@ def tile_list_picked_tokens_by_picked_classes_pl_kernel(
     nc = tc.nc
     with ExitStack() as ctx:
         keep = ctx.enter_context(tc.tile_pool(name="keep", bufs=1))
-        ring = ctx.enter_context(tc.tile_pool(name="ring", bufs=RING))
+        ring = ctx.enter_context(tc.tile_pool(name="ring", bufs=1))
         psum = ctx.enter_context(tc.psum_pool(name="psum", bufs=1))
 
         tok = keep.tile([P, J // 16], U16, name="tok")
@@ -48,16 +47,16 @@ def tile_list_picked_tokens_by_picked_classes_pl_kernel(
         ident = keep.tile([P, P], F32, name="ident")
         s1 = keep.tile([P, I], U8, name="s1", align_bytes=64)
 
-        nc.gpsimd.memset(swin[:].bitcast(I32), 0)
-        nc.vector.memset(cbwin[:], 0.0)
+        nc.vector.memset(swin[:].bitcast(I32), 0)
+        nc.gpsimd.memset(cbwin[:], 0.0)
         nc.vector.memset(warm[:], 0.0)
-        nc.vector.memset(s1[:].bitcast(I32), 0)
+        nc.gpsimd.memset(s1[:].bitcast(I32), 0)
 
         xrows = xa.rearrange("(g p h e) t -> g h p e t", g=PASSES, p=P, h=2, e=2)
 
         def load_x(n):
             q, c = divmod(n, T // CHUNK)
-            raw[q, c] = ring.tile([P, 2, CHUNK], F32, name="raw")
+            raw[q, c] = ring.tile([P, 2, CHUNK], F32, name=f"raw{n}", tag=f"slot{n}")
             nc.sync.dma_start(raw[q, c][:], xrows[q // 2, q % 2][:, :, c * CHUNK : (c + 1) * CHUNK])
 
         nc.sync.dma_start(cls[:], offs2)
@@ -68,35 +67,30 @@ def tile_list_picked_tokens_by_picked_classes_pl_kernel(
                 swin[32 * Q : 32 * Q + 4 * PASSES, :].bitcast(I32),
                 wc_scales[:, 4 * Q : 4 * Q + 4, :].bitcast(I32),
             )
-        nc.sync.dma_start(wwin[1][:].bitcast(I32), wc_words[1].bitcast(I32))
-        load_x(1)
-        nc.sync.dma_start(tok[:], offs)
         nc.scalar.dma_start(cbwin[0:1, :], cb[0:1, :])
-        for n in range(2, RING):
+        load_x(1)
+        nc.sync.dma_start(wwin[1][:].bitcast(I32), wc_words[1].bitcast(I32))
+        nc.sync.dma_start(tok[:], offs)
+        for n in range(2, 8):
             load_x(n)
         nc.scalar.activation(warm2[:], warm[:], TANH)
         make_identity(nc, ident[:])
 
         wg = [keep.tile([P, I], U16, name=f"wg{g}", align_bytes=64) for g in range(PASSES)]
         sg = keep.tile([P, I], U8, name="sg", align_bytes=64)
-        bias = keep.tile([P, I], F32, name="bias")
         nc.vector.tensor_copy(wg[0][:], wwin[0][:].indirect(cls[:]))
         nc.vector.tensor_copy(sg[:], swin[:].indirect(cls[:]))
         for Q in range(4):
-            nc.gpsimd.dma_start(
+            nc.sync.dma_start(
                 s1[32 * Q : 32 * Q + 4, :].bitcast(I32), sg[32 * Q + 4 : 32 * Q + 8, :].bitcast(I32)
             )
-        nc.vector.tensor_copy(wg[1][:], wwin[1][:].indirect(cls[:]))
         biasrow = keep.tile([P, I], F32, name="biasrow")
-        biascol = keep.tile([P, I // P], F32, name="biascol")
         nc.vector.tensor_copy(biasrow[:], cbwin[:].indirect(cls[:]))
-        turned = psum.tile([P, I // P, P], F32, name="turned")
+        nc.vector.tensor_copy(wg[1][:], wwin[1][:].indirect(cls[:]))
+        turned = psum.tile([P, I // P, P], F32, name="turned", tag="acc0")
         spread = psum.tile([P, I // P, P], F32, name="spread")
         for b in range(I // P):
             nc.tensor.transpose(turned[:, b, :], biasrow[:, b * P : (b + 1) * P], ident[:])
-        nc.scalar.copy(biascol[:], turned[:, :, 0])
-        for b in range(I // P):
-            nc.tensor.transpose(spread[:, b, :], biascol[:, b : b + 1].to_broadcast([P, P]), ident[:])
         wscale = [sg, s1]
 
         def cast(eng, q, lo, hi):
@@ -106,27 +100,31 @@ def tile_list_picked_tokens_by_picked_classes_pl_kernel(
                 raw[q, c][:, :, at : at + hi - lo].rearrange("p e t -> p t e"),
             )
 
-        HALF = J // 2
+        PARTS = (1, 2)
         picked = [
-            [keep.tile([P, 2, HALF], F32, name=f"picked{g}_{s}") for s in range(2)] for g in range(PASSES)
+            [keep.tile([P, 2, J // PARTS[g]], F32, name=f"picked{g}_{s}") for s in range(PARTS[g])]
+            for g in range(PASSES)
         ]
         grouped = [keep.tile([P, PACK * J], BF16, name=f"grouped{g}", align_bytes=64) for g in range(PASSES)]
         codes = [keep.tile([P, J], U32, name=f"codes{g}", align_bytes=64) for g in range(PASSES)]
         scales = [keep.tile([P, J], U8, name=f"scales{g}", align_bytes=64) for g in range(PASSES)]
-        acc = [psum.tile([P, I], F32, name=f"acc{t}") for t in range(PACK)]
+
+        acc = []
 
         def gather(q, s):
+            n = J // 16 // PARTS[q // 2]
             nc.vector.tensor_copy(
                 picked[q // 2][s][:, q % 2, :],
-                win[q][:].bitcast(F32).indirect(tok[:, s * 16 : (s + 1) * 16]),
+                win[q][:].bitcast(F32).indirect(tok[:, s * n : (s + 1) * n]),
             )
 
         def weave(eng, g, s):
+            n = P // PARTS[g]
             eng(
-                grouped[g][:].bitcast(F32).rearrange("p (t m h) -> p m h t", t=PACK, h=2)[
-                    :, s * 64 : (s + 1) * 64
+                grouped[g][:].bitcast(F32).rearrange("p (t m h) -> p m t h", t=PACK, h=2)[
+                    :, s * n : (s + 1) * n
                 ],
-                picked[g][s][:].rearrange("p h (m t) -> p m h t", t=PACK),
+                picked[g][s][:].rearrange("p h (m t) -> p m t h", t=PACK),
             )
 
         def quant(g, lo, hi):
@@ -150,16 +148,18 @@ def tile_list_picked_tokens_by_picked_classes_pl_kernel(
         for q in range(3):
             for c in range(2):
                 cast(nc.scalar.copy, q, c * CHUNK, (c + 1) * CHUNK)
-                if 2 * q + c + RING < 8:
-                    load_x(2 * q + c + RING)
-            gather(q, 0)
-            gather(q, 1)
+            for s in range(PARTS[q // 2]):
+                gather(q, s)
             if q == 1:
                 weave(nc.vector.tensor_copy, 0, 0)
-                weave(nc.vector.tensor_copy, 0, 1)
                 quant(0, 0, J)
-                for t in range(PACK):
-                    mm(0, t)
+        biascol = ring.tile([P, I // P], F32, name="biascol", tag="slot5")
+        nc.scalar.copy(biascol[:], turned[:, :, 0])
+        for b in range(I // P):
+            nc.tensor.transpose(spread[:, b, :], biascol[:, b : b + 1].to_broadcast([P, P]), ident[:])
+        acc.extend(psum.tile([P, I], F32, name=f"acc{t}", tag=f"acc{t}") for t in range(PACK))
+        for t in range(PACK):
+            mm(0, t)
         cast(nc.scalar.copy, 3, 0, CHUNK)
         cast(nc.scalar.copy, 3, CHUNK, CHUNK + LAST_SCALAR)
         cast(nc.vector.tensor_copy, 3, CHUNK + LAST_SCALAR, T)
@@ -167,6 +167,7 @@ def tile_list_picked_tokens_by_picked_classes_pl_kernel(
         gather(3, 1)
         weave(nc.scalar.copy, 1, 0)
         weave(nc.vector.tensor_copy, 1, 1)
+        bias = ring.tile([P, I], F32, name="bias", tag="slot7")
         nc.scalar.copy(bias[:], spread[:].rearrange("p b n -> p (b n)"))
         for t in range(PACK):
             quant(1, t * P, (t + 1) * P)
@@ -179,12 +180,11 @@ def tile_list_picked_tokens_by_picked_classes_pl_kernel(
         yscales = keep.tile([P, I], U8, name="yscales", align_bytes=64)
         orows = out_0.rearrange("(p t) i -> p t i", t=PACK)
         IH = I // 2
-        for t in range(PACK):
-            spans = [(0, I)] if t < PACK - 1 else [(0, IH), (IH, I)]
-            for lo, hi in spans:
-                nc.vector.tensor_tensor(z[t][:, lo:hi], acc[t][:, lo:hi], bias[:, lo:hi], ADD)
-                nc.scalar.activation(y[:, t, lo:hi], z[t][:, lo:hi], TANH)
-            nc.sync.dma_start(orows[:, t, :], y[:, t, :])
+        for t, lo, hi in [(0, 0, I), (1, 0, I), (2, 0, IH), (3, 0, IH), (2, IH, I), (3, IH, I)]:
+            nc.vector.tensor_tensor(z[t][:, lo:hi], acc[t][:, lo:hi], bias[:, lo:hi], ADD)
+            nc.scalar.activation(y[:, t, lo:hi], z[t][:, lo:hi], TANH)
+            if hi == I:
+                nc.sync.dma_start(orows[:, t, :], y[:, t, :])
 
         def ycast(eng, lo, hi):
             eng(
@@ -208,7 +208,7 @@ def tile_list_picked_tokens_by_picked_classes_pl_kernel(
         yquant(0, IH)
         yquant(IH, I)
         for Q in range(4):
-            eng = nc.sync if Q < 2 else nc.scalar
+            eng = nc.sync if Q < 1 else nc.scalar
             eng.dma_start(
                 out_2[0, 4 * Q : 4 * Q + 4, :].bitcast(I32), yscales[32 * Q : 32 * Q + 4, :].bitcast(I32)
             )

@@ -22,7 +22,8 @@ P = 128
 PACK = 4
 PASSES = K // (P * PACK)
 CHUNK = 512
-LAST_SCALAR = 160
+SPLIT = 320
+LAST_SCALAR = 224
 CAST_SCALAR = 160
 
 
@@ -37,20 +38,20 @@ def tile_list_picked_tokens_by_picked_classes_pl_kernel(
 
         tok = keep.tile([P, J // 16], U16, name="tok")
         cls = keep.tile([P, I // 16], U16, name="cls")
-        wwin = [keep.tile([P, C], U16, name=f"wwin{g}", align_bytes=64) for g in range(PASSES)]
+        wwin = [keep.tile([P, C], U16, name=f"wwin{g}", tag=f"wwin{g}", align_bytes=64) for g in range(PASSES)]
         swin = keep.tile([P, C], U8, name="swin", align_bytes=64)
         cbwin = keep.tile([P, C], F32, name="cbwin")
         raw = {}
         win = [keep.tile([P, 2 * T], BF16, name=f"win{q}", align_bytes=64) for q in range(2 * PASSES)]
-        warm = keep.tile([P, 1], F32, name="warm")
         warm2 = keep.tile([P, 1], F32, name="warm2")
         ident = keep.tile([P, P], F32, name="ident")
-        s1 = keep.tile([P, I], U8, name="s1", align_bytes=64)
+        wscale = [keep.tile([P, I], U8, name=f"wscale{g}", align_bytes=64) for g in range(PASSES)]
 
-        nc.vector.memset(swin[:].bitcast(I32), 0)
-        nc.gpsimd.memset(cbwin[:], 0.0)
-        nc.vector.memset(warm[:], 0.0)
-        nc.gpsimd.memset(s1[:].bitcast(I32), 0)
+        nc.gpsimd.memset(swin[32:64, :].bitcast(I32), 0)
+        nc.gpsimd.memset(swin[64:128, :].bitcast(I32), 0)
+        nc.vector.memset(cbwin[:].bitcast(I32), 0)
+        for g in range(PASSES):
+            nc.gpsimd.memset(wscale[g][:].bitcast(I32), 0)
 
         xrows = xa.rearrange("(g p h e) t -> g h p e t", g=PASSES, p=P, h=2, e=2)
 
@@ -60,38 +61,43 @@ def tile_list_picked_tokens_by_picked_classes_pl_kernel(
             nc.sync.dma_start(raw[q, c][:], xrows[q // 2, q % 2][:, :, c * CHUNK : (c + 1) * CHUNK])
 
         nc.sync.dma_start(cls[:], offs2)
+        nc.sync.dma_start(
+            swin[0 : 16 * PASSES, :].bitcast(I32), wc_scales.rearrange("g q c -> (g q) c").bitcast(I32)
+        )
         nc.sync.dma_start(wwin[0][:].bitcast(I32), wc_words[0].bitcast(I32))
         load_x(0)
-        for Q in range(4):
-            nc.scalar.dma_start(
-                swin[32 * Q : 32 * Q + 4 * PASSES, :].bitcast(I32),
-                wc_scales[:, 4 * Q : 4 * Q + 4, :].bitcast(I32),
-            )
-        nc.scalar.dma_start(cbwin[0:1, :], cb[0:1, :])
-        load_x(1)
         nc.sync.dma_start(wwin[1][:].bitcast(I32), wc_words[1].bitcast(I32))
+        nc.sync.dma_start(cbwin[0:1, :], cb[0:1, :])
+        load_x(1)
         nc.sync.dma_start(tok[:], offs)
-        for n in range(2, 8):
+        for n in range(2, 6):
             load_x(n)
-        nc.scalar.activation(warm2[:], warm[:], TANH)
         make_identity(nc, ident[:])
+        nc.scalar.activation(warm2[:], ident[:, 0:1], TANH)
 
         wg = [keep.tile([P, I], U16, name=f"wg{g}", align_bytes=64) for g in range(PASSES)]
         sg = keep.tile([P, I], U8, name="sg", align_bytes=64)
-        nc.vector.tensor_copy(wg[0][:], wwin[0][:].indirect(cls[:]))
         nc.vector.tensor_copy(sg[:], swin[:].indirect(cls[:]))
-        for Q in range(4):
-            nc.sync.dma_start(
-                s1[32 * Q : 32 * Q + 4, :].bitcast(I32), sg[32 * Q + 4 : 32 * Q + 8, :].bitcast(I32)
-            )
-        biasrow = keep.tile([P, I], F32, name="biasrow")
-        nc.vector.tensor_copy(biasrow[:], cbwin[:].indirect(cls[:]))
+        nc.vector.tensor_copy(wg[0][:], wwin[0][:].indirect(cls[:]))
+
+        def place_scales(g):
+            for Q in range(4):
+                row = 16 * g + 4 * Q
+                nc.sync.dma_start(
+                    wscale[g][32 * Q : 32 * Q + 4, :].bitcast(I32), sg[row : row + 4, :].bitcast(I32)
+                )
+
+        place_scales(0)
+        load_x(6)
+        load_x(7)
+        place_scales(1)
         nc.vector.tensor_copy(wg[1][:], wwin[1][:].indirect(cls[:]))
+        biasrow = keep.tile([P, I], F32, name="biasrow", tag="wwin1", align_bytes=64)
+        nc.vector.tensor_copy(biasrow[:], cbwin[:].indirect(cls[:]))
         turned = psum.tile([P, I // P, P], F32, name="turned", tag="acc0")
         spread = psum.tile([P, I // P, P], F32, name="spread")
         for b in range(I // P):
             nc.tensor.transpose(turned[:, b, :], biasrow[:, b * P : (b + 1) * P], ident[:])
-        wscale = [sg, s1]
 
         def cast(eng, q, lo, hi):
             c, at = divmod(lo, CHUNK)
@@ -100,31 +106,25 @@ def tile_list_picked_tokens_by_picked_classes_pl_kernel(
                 raw[q, c][:, :, at : at + hi - lo].rearrange("p e t -> p t e"),
             )
 
-        PARTS = (1, 2)
-        picked = [
-            [keep.tile([P, 2, J // PARTS[g]], F32, name=f"picked{g}_{s}") for s in range(PARTS[g])]
-            for g in range(PASSES)
-        ]
+        picked = [keep.tile([P, 2, J], F32, name=f"picked{g}") for g in range(PASSES)]
         grouped = [keep.tile([P, PACK * J], BF16, name=f"grouped{g}", align_bytes=64) for g in range(PASSES)]
         codes = [keep.tile([P, J], U32, name=f"codes{g}", align_bytes=64) for g in range(PASSES)]
         scales = [keep.tile([P, J], U8, name=f"scales{g}", align_bytes=64) for g in range(PASSES)]
 
         acc = []
 
-        def gather(q, s):
-            n = J // 16 // PARTS[q // 2]
+        def gather(q, lo, hi):
             nc.vector.tensor_copy(
-                picked[q // 2][s][:, q % 2, :],
-                win[q][:].bitcast(F32).indirect(tok[:, s * n : (s + 1) * n]),
+                picked[q // 2][:, q % 2, lo:hi],
+                win[q][:].bitcast(F32).indirect(tok[:, lo // 16 : hi // 16]),
             )
 
-        def weave(eng, g, s):
-            n = P // PARTS[g]
+        def weave(eng, g, lo, hi):
             eng(
                 grouped[g][:].bitcast(F32).rearrange("p (t m h) -> p m t h", t=PACK, h=2)[
-                    :, s * n : (s + 1) * n
+                    :, lo // PACK : hi // PACK
                 ],
-                picked[g][s][:].rearrange("p h (m t) -> p m t h", t=PACK),
+                picked[g][:, :, lo:hi].rearrange("p h (m t) -> p m t h", t=PACK),
             )
 
         def quant(g, lo, hi):
@@ -148,25 +148,24 @@ def tile_list_picked_tokens_by_picked_classes_pl_kernel(
         for q in range(3):
             for c in range(2):
                 cast(nc.scalar.copy, q, c * CHUNK, (c + 1) * CHUNK)
-            for s in range(PARTS[q // 2]):
-                gather(q, s)
+            gather(q, 0, J)
             if q == 1:
-                weave(nc.vector.tensor_copy, 0, 0)
+                weave(nc.vector.tensor_copy, 0, 0, J)
                 quant(0, 0, J)
-        biascol = ring.tile([P, I // P], F32, name="biascol", tag="slot5")
+        cast(nc.scalar.copy, 3, 0, CHUNK)
+        biascol = ring.tile([P, I // P], F32, name="biascol", tag="slot6")
         nc.scalar.copy(biascol[:], turned[:, :, 0])
         for b in range(I // P):
             nc.tensor.transpose(spread[:, b, :], biascol[:, b : b + 1].to_broadcast([P, P]), ident[:])
         acc.extend(psum.tile([P, I], F32, name=f"acc{t}", tag=f"acc{t}") for t in range(PACK))
         for t in range(PACK):
             mm(0, t)
-        cast(nc.scalar.copy, 3, 0, CHUNK)
         cast(nc.scalar.copy, 3, CHUNK, CHUNK + LAST_SCALAR)
         cast(nc.vector.tensor_copy, 3, CHUNK + LAST_SCALAR, T)
-        gather(3, 0)
-        gather(3, 1)
-        weave(nc.scalar.copy, 1, 0)
-        weave(nc.vector.tensor_copy, 1, 1)
+        gather(3, 0, SPLIT)
+        gather(3, SPLIT, J)
+        weave(nc.scalar.copy, 1, 0, SPLIT)
+        weave(nc.vector.tensor_copy, 1, SPLIT, J)
         bias = ring.tile([P, I], F32, name="bias", tag="slot7")
         nc.scalar.copy(bias[:], spread[:].rearrange("p b n -> p (b n)"))
         for t in range(PACK):
@@ -180,11 +179,22 @@ def tile_list_picked_tokens_by_picked_classes_pl_kernel(
         yscales = keep.tile([P, I], U8, name="yscales", align_bytes=64)
         orows = out_0.rearrange("(p t) i -> p t i", t=PACK)
         IH = I // 2
-        for t, lo, hi in [(0, 0, I), (1, 0, I), (2, 0, IH), (3, 0, IH), (2, IH, I), (3, IH, I)]:
+        def finish(t, lo, hi):
             nc.vector.tensor_tensor(z[t][:, lo:hi], acc[t][:, lo:hi], bias[:, lo:hi], ADD)
             nc.scalar.activation(y[:, t, lo:hi], z[t][:, lo:hi], TANH)
-            if hi == I:
-                nc.sync.dma_start(orows[:, t, :], y[:, t, :])
+
+        def store(t0, t1, lo, hi):
+            nc.sync.dma_start(orows[:, t0:t1, lo:hi], y[:, t0:t1, lo:hi])
+
+        for lo, hi in [(0, IH), (IH, I)]:
+            finish(0, lo, hi)
+            store(0, 1, lo, hi)
+        finish(1, 0, I)
+        store(1, 2, 0, I)
+        for lo, hi in [(0, IH), (IH, I)]:
+            finish(2, lo, hi)
+            finish(3, lo, hi)
+            store(2, 4, lo, hi)
 
         def ycast(eng, lo, hi):
             eng(

@@ -43,7 +43,6 @@ def tile_list_picked_tokens_by_picked_classes_pl_kernel(
         cbwin = keep.tile([P, C], F32, name="cbwin")
         raw = {}
         win = [keep.tile([P, 2 * T], BF16, name=f"win{q}", align_bytes=64) for q in range(2 * PASSES)]
-        warm2 = keep.tile([P, 1], F32, name="warm2")
         ident = keep.tile([P, P], F32, name="ident")
         wscale = [keep.tile([P, I], U8, name=f"wscale{g}", align_bytes=64) for g in range(PASSES)]
 
@@ -73,7 +72,6 @@ def tile_list_picked_tokens_by_picked_classes_pl_kernel(
         for n in range(2, 6):
             load_x(n)
         make_identity(nc, ident[:])
-        nc.scalar.activation(warm2[:], ident[:, 0:1], TANH)
 
         wg = [keep.tile([P, I], U16, name=f"wg{g}", align_bytes=64) for g in range(PASSES)]
         sg = keep.tile([P, I], U8, name="sg", align_bytes=64)

from contextlib import ExitStack

import concourse.mybir as mybir
from concourse.masks import make_identity

K, T, C, J, I = 1024, 1024, 1024, 512, 512
FLOPS = 2 * K * J * I
BYTES = 4 * K * T + K * C // 2 + K * C // 32 + 4 * C + 2 * 2 * 128 * 32 + 4 * J * I + J * I + J * I // 32

F32 = mybir.dt.float32
BF16 = mybir.dt.bfloat16
I32 = mybir.dt.int32
U32 = mybir.dt.uint32
U16 = mybir.dt.uint16
U8 = mybir.dt.uint8
FP8X4 = mybir.dt.float8_e4m3fn_x4
FP4X4 = mybir.dt.float4_e2m1fn_x4
TANH = mybir.ActivationFunctionType.Tanh
ADD = mybir.AluOpType.add

P = 128
PACK = 4
PASSES = K // (P * PACK)
CHUNK = 512
SPLIT = 320
LAST_SCALAR = 224
CAST_SCALAR = 160


def tile_list_picked_tokens_by_picked_classes_pl_kernel(
    tc, xa, wc_words, wc_scales, cb, offs, offs2, out_0, out_1, out_2
):
    nc = tc.nc
    with ExitStack() as ctx:
        keep = ctx.enter_context(tc.tile_pool(name="keep", bufs=1))
        ring = ctx.enter_context(tc.tile_pool(name="ring", bufs=1))
        psum = ctx.enter_context(tc.psum_pool(name="psum", bufs=1))

        tok = keep.tile([P, J // 16], U16, name="tok")
        cls = keep.tile([P, I // 16], U16, name="cls")
        wwin = [keep.tile([P, C], U16, name=f"wwin{g}", tag=f"wwin{g}", align_bytes=64) for g in range(PASSES)]
        swin = keep.tile([P, C], U8, name="swin", align_bytes=64)
        cbwin = keep.tile([P, C], F32, name="cbwin")
        raw = {}
        win = [keep.tile([P, 2 * T], BF16, name=f"win{q}", align_bytes=64) for q in range(2 * PASSES)]
        ident = keep.tile([P, P], F32, name="ident")
        wscale = [keep.tile([P, I], U8, name=f"wscale{g}", align_bytes=64) for g in range(PASSES)]

        nc.gpsimd.memset(swin[32:64, :].bitcast(I32), 0)
        nc.gpsimd.memset(swin[64:128, :].bitcast(I32), 0)
        nc.vector.memset(cbwin[:].bitcast(I32), 0)
        for g in range(PASSES):
            nc.gpsimd.memset(wscale[g][:].bitcast(I32), 0)

        xrows = xa.rearrange("(g p h e) t -> g h p e t", g=PASSES, p=P, h=2, e=2)

        def load_x(n):
            q, c = divmod(n, T // CHUNK)
            raw[q, c] = ring.tile([P, 2, CHUNK], F32, name=f"raw{n}", tag=f"slot{n}")
            nc.sync.dma_start(raw[q, c][:], xrows[q // 2, q % 2][:, :, c * CHUNK : (c + 1) * CHUNK])

        nc.sync.dma_start(cls[:], offs2)
        nc.sync.dma_start(
            swin[0 : 16 * PASSES, :].bitcast(I32), wc_scales.rearrange("g q c -> (g q) c").bitcast(I32)
        )
        nc.sync.dma_start(wwin[0][:].bitcast(I32), wc_words[0].bitcast(I32))
        load_x(0)
        nc.sync.dma_start(wwin[1][:].bitcast(I32), wc_words[1].bitcast(I32))
        nc.sync.dma_start(cbwin[0:1, :], cb[0:1, :])
        load_x(1)
        nc.sync.dma_start(tok[:], offs)
        for n in range(2, 6):
            load_x(n)
        make_identity(nc, ident[:])

        wg = [keep.tile([P, I], U16, name=f"wg{g}", align_bytes=64) for g in range(PASSES)]
        sg = keep.tile([P, I], U8, name="sg", align_bytes=64)
        nc.vector.tensor_copy(sg[:], swin[:].indirect(cls[:]))
        nc.vector.tensor_copy(wg[0][:], wwin[0][:].indirect(cls[:]))

        def place_scales(g):
            for Q in range(4):
                row = 16 * g + 4 * Q
                nc.sync.dma_start(
                    wscale[g][32 * Q : 32 * Q + 4, :].bitcast(I32), sg[row : row + 4, :].bitcast(I32)
                )

        place_scales(0)
        load_x(6)
        load_x(7)
        place_scales(1)
        nc.vector.tensor_copy(wg[1][:], wwin[1][:].indirect(cls[:]))
        biasrow = keep.tile([P, I], F32, name="biasrow", tag="wwin1", align_bytes=64)
        nc.vector.tensor_copy(biasrow[:], cbwin[:].indirect(cls[:]))
        turned = psum.tile([P, I // P, P], F32, name="turned", tag="acc0")
        spread = psum.tile([P, I // P, P], F32, name="spread")
        for b in range(I // P):
            nc.tensor.transpose(turned[:, b, :], biasrow[:, b * P : (b + 1) * P], ident[:])

        def cast(eng, q, lo, hi):
            c, at = divmod(lo, CHUNK)
            eng(
                win[q][:, 2 * lo : 2 * hi].rearrange("p (t e) -> p t e", e=2),
                raw[q, c][:, :, at : at + hi - lo].rearrange("p e t -> p t e"),
            )

        picked = [keep.tile([P, 2, J], F32, name=f"picked{g}") for g in range(PASSES)]
        grouped = [keep.tile([P, PACK * J], BF16, name=f"grouped{g}", align_bytes=64) for g in range(PASSES)]
        codes = [keep.tile([P, J], U32, name=f"codes{g}", align_bytes=64) for g in range(PASSES)]
        scales = [keep.tile([P, J], U8, name=f"scales{g}", align_bytes=64) for g in range(PASSES)]

        acc = []

        def gather(q, lo, hi):
            nc.vector.tensor_copy(
                picked[q // 2][:, q % 2, lo:hi],
                win[q][:].bitcast(F32).indirect(tok[:, lo // 16 : hi // 16]),
            )

        def weave(eng, g, lo, hi):
            eng(
                grouped[g][:].bitcast(F32).rearrange("p (t m h) -> p m t h", t=PACK, h=2)[
                    :, lo // PACK : hi // PACK
                ],
                picked[g][:, :, lo:hi].rearrange("p h (m t) -> p m t h", t=PACK),
            )

        def quant(g, lo, hi):
            nc.vector.quantize_mx(
                out=codes[g][:, lo:hi].bitcast(FP8X4),
                scales=scales[g][:, lo:hi],
                in_=grouped[g][:, PACK * lo : PACK * hi],
            )

        def mm(g, t):
            nc.tensor.matmul_mx(
                out=acc[t][:],
                lhsT=codes[g][:, t * P : (t + 1) * P].bitcast(FP8X4),
                lhsT_scale=scales[g][:, t * P : (t + 1) * P],
                rhs=wg[g][:].bitcast(FP4X4),
                rhs_scale=wscale[g][:],
                start=(g == 0),
                stop=(g == PASSES - 1),
            )

        for q in range(3):
            for c in range(2):
                cast(nc.scalar.copy, q, c * CHUNK, (c + 1) * CHUNK)
            gather(q, 0, J)
            if q == 1:
                weave(nc.vector.tensor_copy, 0, 0, J)
                quant(0, 0, J)
        cast(nc.scalar.copy, 3, 0, CHUNK)
        biascol = ring.tile([P, I // P], F32, name="biascol", tag="slot6")
        nc.scalar.copy(biascol[:], turned[:, :, 0])
        for b in range(I // P):
            nc.tensor.transpose(spread[:, b, :], biascol[:, b : b + 1].to_broadcast([P, P]), ident[:])
        acc.extend(psum.tile([P, I], F32, name=f"acc{t}", tag=f"acc{t}") for t in range(PACK))
        for t in range(PACK):
            mm(0, t)
        cast(nc.scalar.copy, 3, CHUNK, CHUNK + LAST_SCALAR)
        cast(nc.vector.tensor_copy, 3, CHUNK + LAST_SCALAR, T)
        gather(3, 0, SPLIT)
        gather(3, SPLIT, J)
        weave(nc.scalar.copy, 1, 0, SPLIT)
        weave(nc.vector.tensor_copy, 1, SPLIT, J)
        bias = ring.tile([P, I], F32, name="bias", tag="slot7")
        nc.scalar.copy(bias[:], spread[:].rearrange("p b n -> p (b n)"))
        for t in range(PACK):
            quant(1, t * P, (t + 1) * P)
            mm(1, t)

        y = keep.tile([P, PACK, I], F32, name="y")
        z = [keep.tile([P, I], F32, name=f"z{t}") for t in range(PACK)]
        yb = keep.tile([P, PACK * I], BF16, name="yb", align_bytes=64)
        ycodes = keep.tile([P, I], U32, name="ycodes", align_bytes=64)
        yscales = keep.tile([P, I], U8, name="yscales", align_bytes=64)
        orows = out_0.rearrange("(p t) i -> p t i", t=PACK)
        IH = I // 2
        def finish(t, lo, hi):
            nc.vector.tensor_tensor(z[t][:, lo:hi], acc[t][:, lo:hi], bias[:, lo:hi], ADD)
            nc.scalar.activation(y[:, t, lo:hi], z[t][:, lo:hi], TANH)

        def store(t0, t1, lo, hi):
            nc.sync.dma_start(orows[:, t0:t1, lo:hi], y[:, t0:t1, lo:hi])

        for lo, hi in [(0, IH), (IH, I)]:
            finish(0, lo, hi)
            store(0, 1, lo, hi)
        finish(1, 0, I)
        store(1, 2, 0, I)
        for lo, hi in [(0, IH), (IH, I)]:
            finish(2, lo, hi)
            finish(3, lo, hi)
            store(2, 4, lo, hi)

        def ycast(eng, lo, hi):
            eng(
                yb[:, PACK * lo : PACK * hi].rearrange("p (c i t) -> p c t i", i=4, t=PACK),
                y[:, :, lo:hi].rearrange("p t (c i) -> p c t i", i=4),
            )

        owords = out_1[0].rearrange("p c r -> p (c r)").bitcast(I32)

        def yquant(lo, hi):
            nc.vector.quantize_mx(
                out=ycodes[:, lo:hi].bitcast(FP8X4),
                scales=yscales[:, lo:hi],
                in_=yb[:, PACK * lo : PACK * hi],
            )
            nc.sync.dma_start(owords[:, lo:hi], ycodes[:, lo:hi].bitcast(I32))

        ycast(nc.vector.tensor_copy, 0, IH)
        ycast(nc.scalar.copy, I - CAST_SCALAR, I)
        ycast(nc.vector.tensor_copy, IH, I - CAST_SCALAR)
        yquant(0, IH)
        yquant(IH, I)
        for Q in range(4):
            eng = nc.sync if Q < 1 else nc.scalar
            eng.dma_start(
                out_2[0, 4 * Q : 4 * Q + 4, :].bitcast(I32), yscales[32 * Q : 32 * Q + 4, :].bitcast(I32)
            )
